import numpy as np
import ml_dtypes


def mxq(x, axis, fmt="e4m3"):
    dtype, down = {"e4m3": (ml_dtypes.float8_e4m3fn, 7), "e5m2": (ml_dtypes.float8_e5m2, 14)}[fmt]
    v = np.moveaxis(np.asarray(x, np.float32).astype(ml_dtypes.bfloat16).astype(np.float64), axis, -1)
    blocks = v.reshape(v.shape[:-1] + (-1, 32))
    amax = np.abs(blocks).max(-1, keepdims=True)
    byte = np.maximum(np.where(amax > 0, np.frexp(amax)[1] - 1 + 127, 0) - down, 1)
    scale = np.exp2(byte - 127.0)
    codes = (blocks / scale).astype(np.float32).astype(dtype).astype(np.float64)
    return np.moveaxis((codes * scale).reshape(v.shape), -1, axis)


WIDE = False


def mx_kscale(k):
    if not WIDE:
        return np.ones(k)
    levels = np.array([30, -30])
    if k % 512:
        return np.exp2(np.random.permutation(np.resize(levels, k // 32))).repeat(32)
    a = np.empty((k // 512, 16))
    for p in range(k // 512):
        a[p, :8] = np.random.permutation(np.resize(levels, 8))
        for g in range(8):
            far = levels[np.abs(levels - a[p, g]) >= 10]
            a[p, g + 8] = far[np.random.randint(len(far))]
    return np.exp2(a.ravel()).repeat(32)


BF16 = ml_dtypes.bfloat16


def bf(x):
    return np.asarray(x, np.float32).astype(BF16)


def f64(x):
    return np.asarray(x).astype(np.float64)


N, A, B, M = 2048, 1024, 512, 1536


def setup_inputs():
    s, t = mx_kscale(A), mx_kscale(B)
    phi = np.random.standard_normal((M, N))
    g = np.random.standard_normal((M, M))
    d = np.exp(np.concatenate([0.2 * np.random.standard_normal(A), 0.5 * np.random.standard_normal(B)]))
    c = (np.eye(M) + 0.45 * (g + g.T) / np.sqrt(2 * M)) * d[:, None] * d
    return {"phi_a": bf(phi[:A] * s[:, None]),
            "phi_b": bf(phi[A:] * t[:, None]),
            "prec_a": bf(c[:A] / s[:, None]),
            "prec_b": bf(c[A:] / t[:, None]),
            "atoms": bf(phi.T / M),
            "gamma": bf(0.2 + 0.4 * np.random.random(N))}


def reference(phi_a, phi_b, prec_a, prec_b, atoms, gamma):
    prior = f64(gamma)
    pa = mxq(f64(phi_a), 0, "e4m3")
    ca = mxq(f64(prec_a), 0, "e4m3")
    pb = mxq(f64(phi_b), 0, "e4m3")
    cb = mxq(f64(prec_b), 0, "e5m2")
    proj = (pa.T @ ca) + (pb.T @ cb)
    gain = prior[:, None] * proj
    explained = (gain * f64(atoms)).sum(axis=1)
    var = prior - prior * explained
    return gain, var

@@ -1,0 +1,206 @@
+from contextlib import ExitStack
+
+import concourse.mybir as mybir
+from concourse.masks import make_identity
+
+N_ATOMS, N_SENSORS = 2048, 1536
+FLOPS = 2 * N_ATOMS * N_SENSORS * N_SENSORS
+
+F32 = mybir.dt.float32
+BF16 = mybir.dt.bfloat16
+U32 = mybir.dt.uint32
+U8 = mybir.dt.uint8
+E4M3 = mybir.dt.float8_e4m3fn_x4
+E5M2 = mybir.dt.float8_e5m2_x4
+ALU = mybir.AluOpType
+COPY = mybir.ActivationFunctionType.Copy
+
+P = 128
+PACK = 4
+K_PASS = P * PACK
+PASSES = 3
+W = 512
+ROW_TILES = N_ATOMS // P
+COL_TILES = N_SENSORS // W
+GROUP = W // P
+
+S_HEAD = 256
+S_MID = 160
+S_LATE = 280
+
+
+def tile_sparse_bayes_posterior_variance_s2_kernel(
+    tc, phi_a, phi_b, prec_a, prec_b, atoms, gamma, out_0, out_1
+):
+    nc = tc.nc
+
+    def source(kind, b, g):
+        first, second = (phi_a, phi_b) if kind == "phi" else (prec_a, prec_b)
+        rows = first[g * K_PASS : (g + 1) * K_PASS, :] if g < 2 else second
+        return rows[:, b * W : (b + 1) * W].rearrange("(p j) w -> p j w", j=PACK)
+
+    def fmt(kind, g):
+        return E5M2 if (kind == "prec" and g == 2) else E4M3
+
+    chunks = []
+    for g in range(PASSES):
+        chunks.extend([("prec", 0, g), ("phi", 0, g)])
+    for kind, b in (("prec", 1), ("prec", 2), ("phi", 1), ("phi", 2), ("phi", 3)):
+        chunks.extend([(kind, b, g) for g in range(PASSES)])
+
+    with ExitStack() as ctx:
+        keep = ctx.enter_context(tc.tile_pool(name="keep", bufs=1))
+        stream = ctx.enter_context(tc.tile_pool(name="stream", bufs=1))
+        psum = ctx.enter_context(tc.psum_pool(name="psum", bufs=8))
+        ctx.enter_context(tc.manual_schedule())
+
+        raw, grouped, codes, scales = {}, {}, {}, {}
+        atom_rows, gain, acc = {}, {}, {}
+
+        def load_chunk(c):
+            t = stream.tile([P, PACK, W], BF16, name="raw", tag="raw", bufs=15)
+            nc.sync.dma_start(out=t[:], in_=source(*chunks[c]))
+            raw[c] = t
+
+        def load_atoms(a):
+            t = stream.tile([P, 2, N_SENSORS], BF16, name="atom_rows", tag="atom_rows", bufs=5)
+            rows = atoms[2 * P * a : 2 * P * (a + 1), :]
+            nc.sync.dma_start(out=t[:], in_=rows.rearrange("(h p) s -> p h s", p=P))
+            atom_rows[a] = t
+
+        def interleave(c, s_cols):
+            t = stream.tile([P, W, PACK], BF16, name="grouped", tag="grouped", bufs=4, align_bytes=64)
+            src = raw[c][:].rearrange("p j w -> p w j")
+            v_cols = W - s_cols
+            nc.scalar.copy(out=t[:, v_cols:, :], in_=src[:, v_cols:, :])
+            nc.vector.tensor_copy(out=t[:, :v_cols, :], in_=src[:, :v_cols, :])
+            grouped[c] = t
+
+        def quantize(c):
+            kind, b, g = chunks[c]
+            cw = keep.tile([P, W], U32, name="codes_%d" % c, align_bytes=64)
+            sc = keep.tile([P, W], U8, name="scales_%d" % c, align_bytes=64)
+            nc.vector.quantize_mx(
+                out=cw[:].bitcast(fmt(kind, g)),
+                scales=sc[:],
+                in_=grouped[c][:].rearrange("p w j -> p (w j)"),
+            )
+            codes[chunks[c]], scales[chunks[c]] = cw, sc
+
+        def mx_pass(m, n, g):
+            if g == 0:
+                acc[(m, n)] = psum.tile([P, W], F32, name="bank", tag="bank")
+            left, right = ("phi", m // GROUP, g), ("prec", n, g)
+            cols = slice((m % GROUP) * P, (m % GROUP + 1) * P)
+            nc.tensor.matmul_mx(
+                out=acc[(m, n)][:],
+                lhsT=codes[left][:, cols].bitcast(E4M3),
+                lhsT_scale=scales[left][:, cols],
+                rhs=codes[right][:].bitcast(fmt("prec", g)),
+                rhs_scale=scales[right][:],
+                start=(g == 0),
+                stop=(g == PASSES - 1),
+            )
+
+        def group_pass(b, n, g):
+            for m in range(b * GROUP, (b + 1) * GROUP):
+                mx_pass(m, n, g)
+
+        def drain(m, n):
+            if n == 0:
+                gain[m] = stream.tile([P, N_SENSORS], F32, name="gain", tag="gain", bufs=9)
+            nc.scalar.activation(
+                out=gain[m][:, n * W : (n + 1) * W], in_=acc[(m, n)][:], func=COPY, scale=prior[:, m : m + 1]
+            )
+
+        def store(m):
+            nc.sync.dma_start(out=out_0[m * P : (m + 1) * P, :], in_=gain[m][:])
+
+        def explain(m):
+            products = stream.tile([P, N_SENSORS], F32, name="products", tag="products", bufs=2)
+            nc.vector.scalar_tensor_tensor(
+                out=products[:],
+                in0=gain[m][:],
+                scalar=1.0,
+                in1=atom_rows[m // 2][:, m % 2, :],
+                op0=ALU.mult,
+                op1=ALU.mult,
+                accum_out=explained[:, m : m + 1],
+            )
+
+        gamma_rows = keep.tile([ROW_TILES, P], BF16)
+        nc.scalar.dma_start(out=gamma_rows[:], in_=gamma.rearrange("(m p) -> m p", p=P))
+        for c in range(15):
+            load_chunk(c)
+        load_atoms(0)
+        load_atoms(1)
+        gamma_square = keep.tile([P, P], F32)
+        var_square = keep.tile([P, P], F32)
+        identity = keep.tile([P, P], F32)
+        nc.gpsimd.memset(gamma_square[:], 0.0)
+        make_identity(nc, identity[:])
+        nc.gpsimd.memset(var_square[:], 0.0)
+        nc.scalar.activation(out=gamma_square[:ROW_TILES, :], in_=gamma_rows[:], func=COPY)
+        gamma_turned = psum.tile([P, P], F32, name="bank", tag="bank")
+        nc.tensor.transpose(gamma_turned[:], gamma_square[:], identity[:])
+        prior = keep.tile([P, ROW_TILES], F32)
+        explained = keep.tile([P, ROW_TILES], F32)
+
+        units = [(0, 0), (0, 1), (0, 2), (1, 0)]
+        for r in range(16):
+            if r < 15:
+                interleave(r, S_HEAD if r < 7 else S_MID)
+            if r == 1:
+                nc.scalar.copy(out=prior[:], in_=gamma_turned[:, :ROW_TILES])
+            if r >= 1:
+                quantize(r - 1)
+            if r == 15:
+                explain(0)
+            if r == 3:
+                for c in range(15, 18):
+                    load_chunk(c)
+                load_atoms(2)
+            if r in (2, 4, 6):
+                group_pass(0, 0, r // 2 - 1)
+            if r >= 7:
+                u, g = divmod(r - 7, PASSES)
+                if g < 2:
+                    b, n = units[u]
+                    drain(b * GROUP + 2 * g, n)
+                    drain(b * GROUP + 2 * g + 1, n)
+                b, n = units[u + 1]
+                group_pass(b, n, g)
+        store(0)
+        for c in range(18, 21):
+            load_chunk(c)
+
+        for m in range(GROUP, 2 * GROUP):
+            drain(m, 0)
+        for m in range(GROUP, ROW_TILES):
+            c = 15 + 3 * (m // GROUP - 1) + m % GROUP
+            prep = m % GROUP < PASSES and m < 3 * GROUP
+            for n in range(1 if m < 2 * GROUP else 0, COL_TILES):
+                for g in range(PASSES):
+                    mx_pass(m, n, g)
+            if prep:
+                interleave(c, S_LATE)
+            explain(m - 3)
+            if prep:
+                quantize(c)
+            for n in range(1 if m < 2 * GROUP else 0, COL_TILES):
+                drain(m, n)
+            store(m - 3)
+            if m % 2 == 0 and m // 2 + 1 < ROW_TILES // 2:
+                load_atoms(m // 2 + 1)
+        for m in range(ROW_TILES - 3, ROW_TILES):
+            store(m)
+            explain(m)
+
+        shrink = keep.tile([P, ROW_TILES], F32)
+        nc.vector.tensor_tensor(out=shrink[:], in0=explained[:], in1=prior[:], op=ALU.mult)
+        nc.vector.tensor_tensor(out=var_square[:, :ROW_TILES], in0=prior[:], in1=shrink[:], op=ALU.subtract)
+        var_turned = psum.tile([P, P], F32, name="bank", tag="bank")
+        nc.tensor.transpose(var_turned[:], var_square[:], identity[:])
+        var_rows = keep.tile([ROW_TILES, P], F32)
+        nc.scalar.copy(out=var_rows[:], in_=var_turned[:ROW_TILES, :])
+        nc.scalar.dma_start(out=out_1.rearrange("(m p) -> m p", p=P), in_=var_rows[:])

@@ -23,10 +23,14 @@ W = 512
 ROW_TILES = N_ATOMS // P
 COL_TILES = N_SENSORS // W
 GROUP = W // P
+HALF = N_ATOMS // 2
 
 S_HEAD = 256
 S_MID = 160
-S_LATE = 280
+S_LATE = 384
+PE_LEAD = 4
+PREP_FIRST = 16
+PREP_STEP = 4
 
 
 def tile_sparse_bayes_posterior_variance_s2_kernel(
@@ -34,19 +38,11 @@ def tile_sparse_bayes_posterior_variance_s2_kernel(
 ):
     nc = tc.nc
 
-    def source(kind, b, g):
-        first, second = (phi_a, phi_b) if kind == "phi" else (prec_a, prec_b)
-        rows = first[g * K_PASS : (g + 1) * K_PASS, :] if g < 2 else second
-        return rows[:, b * W : (b + 1) * W].rearrange("(p j) w -> p j w", j=PACK)
+    def k_rows(first, second, g):
+        return first[g * K_PASS : (g + 1) * K_PASS, :] if g < 2 else second
 
     def fmt(kind, g):
         return E5M2 if (kind == "prec" and g == 2) else E4M3
-
-    chunks = []
-    for g in range(PASSES):
-        chunks.extend([("prec", 0, g), ("phi", 0, g)])
-    for kind, b in (("prec", 1), ("prec", 2), ("phi", 1), ("phi", 2), ("phi", 3)):
-        chunks.extend([(kind, b, g) for g in range(PASSES)])
 
     with ExitStack() as ctx:
         keep = ctx.enter_context(tc.tile_pool(name="keep", bufs=1))
@@ -57,35 +53,46 @@ def tile_sparse_bayes_posterior_variance_s2_kernel(
         raw, grouped, codes, scales = {}, {}, {}, {}
         atom_rows, gain, acc = {}, {}, {}
 
-        def load_chunk(c):
-            t = stream.tile([P, PACK, W], BF16, name="raw", tag="raw", bufs=15)
-            nc.sync.dma_start(out=t[:], in_=source(*chunks[c]))
-            raw[c] = t
+        def load_phi(h, g):
+            t = stream.tile([P, PACK, HALF], BF16, name="phi_raw", tag="phi_raw", bufs=6)
+            rows = k_rows(phi_a, phi_b, g)[:, h * HALF : (h + 1) * HALF]
+            nc.sync.dma_start(out=t[:], in_=rows.rearrange("(p j) w -> p j w", j=PACK))
+            for b in range(2):
+                raw[("phi", 2 * h + b, g)] = t[:, :, b * W : (b + 1) * W]
 
-        def load_atoms(a):
-            t = stream.tile([P, 2, N_SENSORS], BF16, name="atom_rows", tag="atom_rows", bufs=5)
-            rows = atoms[2 * P * a : 2 * P * (a + 1), :]
+        def load_prec(g):
+            t = stream.tile([P, PACK, N_SENSORS], BF16, name="prec_raw", tag="wide_rows", bufs=4)
+            nc.sync.dma_start(out=t[:], in_=k_rows(prec_a, prec_b, g).rearrange("(p j) w -> p j w", j=PACK))
+            for n in range(COL_TILES):
+                raw[("prec", n, g)] = t[:, :, n * W : (n + 1) * W]
+
+        def load_atoms(b):
+            t = stream.tile([P, GROUP, N_SENSORS], BF16, name="atom_rows", tag="wide_rows", bufs=4)
+            rows = atoms[b * W : (b + 1) * W, :]
             nc.sync.dma_start(out=t[:], in_=rows.rearrange("(h p) s -> p h s", p=P))
-            atom_rows[a] = t
+            atom_rows[b] = t
 
-        def interleave(c, s_cols):
+        def interleave(chunk, s_cols):
             t = stream.tile([P, W, PACK], BF16, name="grouped", tag="grouped", bufs=4, align_bytes=64)
-            src = raw[c][:].rearrange("p j w -> p w j")
             v_cols = W - s_cols
-            nc.scalar.copy(out=t[:, v_cols:, :], in_=src[:, v_cols:, :])
-            nc.vector.tensor_copy(out=t[:, :v_cols, :], in_=src[:, :v_cols, :])
-            grouped[c] = t
+            src = raw[chunk].rearrange("p j (c i) -> p c j i", i=4)
+            dst = t[:].rearrange("p (c i) j -> p c j i", i=4)
+            if s_cols > 0:
+                nc.scalar.copy(out=dst[:, v_cols // 4 :], in_=src[:, v_cols // 4 :])
+            if v_cols > 0:
+                nc.vector.tensor_copy(out=dst[:, : v_cols // 4], in_=src[:, : v_cols // 4])
+            grouped[chunk] = t
 
-        def quantize(c):
-            kind, b, g = chunks[c]
-            cw = keep.tile([P, W], U32, name="codes_%d" % c, align_bytes=64)
-            sc = keep.tile([P, W], U8, name="scales_%d" % c, align_bytes=64)
+        def quantize(chunk):
+            kind, b, g = chunk
+            cw = keep.tile([P, W], U32, name="codes_%s_%d_%d" % chunk, align_bytes=64)
+            sc = keep.tile([P, W], U8, name="scales_%s_%d_%d" % chunk, align_bytes=64)
             nc.vector.quantize_mx(
                 out=cw[:].bitcast(fmt(kind, g)),
                 scales=sc[:],
-                in_=grouped[c][:].rearrange("p w j -> p (w j)"),
+                in_=grouped[chunk][:].rearrange("p w j -> p (w j)"),
             )
-            codes[chunks[c]], scales[chunks[c]] = cw, sc
+            codes[chunk], scales[chunk] = cw, sc
 
         def mx_pass(m, n, g):
             if g == 0:
@@ -102,27 +109,30 @@ def tile_sparse_bayes_posterior_variance_s2_kernel(
                 stop=(g == PASSES - 1),
             )
 
-        def group_pass(b, n, g):
-            for m in range(b * GROUP, (b + 1) * GROUP):
-                mx_pass(m, n, g)
-
         def drain(m, n):
-            if n == 0:
-                gain[m] = stream.tile([P, N_SENSORS], F32, name="gain", tag="gain", bufs=9)
+            if n == 0 and m % 2 == 0:
+                gain[m // 2] = stream.tile([P, 2, N_SENSORS], F32, name="gain", tag="gain", bufs=4)
             nc.scalar.activation(
-                out=gain[m][:, n * W : (n + 1) * W], in_=acc[(m, n)][:], func=COPY, scale=prior[:, m : m + 1]
+                out=gain[m // 2][:, m % 2, n * W : (n + 1) * W],
+                in_=acc[(m, n)][:],
+                func=COPY,
+                scale=prior[:, m : m + 1],
             )
 
-        def store(m):
-            nc.sync.dma_start(out=out_0[m * P : (m + 1) * P, :], in_=gain[m][:])
+        def store_pair(q):
+            rows = out_0[2 * q * P : 2 * (q + 1) * P, :]
+            nc.sync.dma_start(out=rows.rearrange("(h p) s -> p h s", p=P), in_=gain[q][:])
+
+        def store_tile(m):
+            nc.sync.dma_start(out=out_0[m * P : (m + 1) * P, :], in_=gain[m // 2][:, m % 2, :])
 
         def explain(m):
             products = stream.tile([P, N_SENSORS], F32, name="products", tag="products", bufs=2)
             nc.vector.scalar_tensor_tensor(
                 out=products[:],
-                in0=gain[m][:],
+                in0=gain[m // 2][:, m % 2, :],
                 scalar=1.0,
-                in1=atom_rows[m // 2][:, m % 2, :],
+                in1=atom_rows[m // GROUP][:, m % GROUP, :],
                 op0=ALU.mult,
                 op1=ALU.mult,
                 accum_out=explained[:, m : m + 1],
@@ -130,10 +140,12 @@ def tile_sparse_bayes_posterior_variance_s2_kernel(
 
         gamma_rows = keep.tile([ROW_TILES, P], BF16)
         nc.scalar.dma_start(out=gamma_rows[:], in_=gamma.rearrange("(m p) -> m p", p=P))
-        for c in range(15):
-            load_chunk(c)
+        for g in range(PASSES):
+            load_phi(0, g)
+            load_prec(g)
+        for g in range(PASSES):
+            load_phi(1, g)
         load_atoms(0)
-        load_atoms(1)
         gamma_square = keep.tile([P, P], F32)
         var_square = keep.tile([P, P], F32)
         identity = keep.tile([P, P], F32)
@@ -146,54 +158,62 @@ def tile_sparse_bayes_posterior_variance_s2_kernel(
         prior = keep.tile([P, ROW_TILES], F32)
         explained = keep.tile([P, ROW_TILES], F32)
 
-        units = [(0, 0), (0, 1), (0, 2), (1, 0)]
-        for r in range(16):
-            if r < 15:
-                interleave(r, S_HEAD if r < 7 else S_MID)
+        head = []
+        for g in range(PASSES - 1):
+            head.extend([("phi", 0, g), ("phi", 1, g)] + [("prec", n, g) for n in range(COL_TILES)])
+        head.extend([("phi", 0, 2)] + [("prec", n, 2) for n in range(COL_TILES)] + [("phi", 1, 2)])
+
+        order = [(m, n) for n in range(COL_TILES) for m in range(GROUP)]
+        order.extend([(m, n) for m in range(GROUP, ROW_TILES) for n in range(COL_TILES)])
+
+        for r in range(len(head) + 1):
+            if r < len(head):
+                interleave(head[r], S_HEAD if r < len(head) - 2 else S_MID)
             if r == 1:
                 nc.scalar.copy(out=prior[:], in_=gamma_turned[:, :ROW_TILES])
             if r >= 1:
-                quantize(r - 1)
-            if r == 15:
-                explain(0)
-            if r == 3:
-                for c in range(15, 18):
-                    load_chunk(c)
-                load_atoms(2)
-            if r in (2, 4, 6):
-                group_pass(0, 0, r // 2 - 1)
-            if r >= 7:
-                u, g = divmod(r - 7, PASSES)
-                if g < 2:
-                    b, n = units[u]
-                    drain(b * GROUP + 2 * g, n)
-                    drain(b * GROUP + 2 * g + 1, n)
-                b, n = units[u + 1]
-                group_pass(b, n, g)
-        store(0)
-        for c in range(18, 21):
-            load_chunk(c)
+                quantize(head[r - 1])
+                kind, n, g = head[r - 1]
+                if kind == "prec" and n < 2:
+                    for m in range(GROUP):
+                        mx_pass(m, n, g)
+            if r in (len(head) - 2, len(head) - 1):
+                drain(*order[2 * (r - len(head) + 2)])
+                drain(*order[2 * (r - len(head) + 2) + 1])
+        load_atoms(1)
 
-        for m in range(GROUP, 2 * GROUP):
-            drain(m, 0)
-        for m in range(GROUP, ROW_TILES):
-            c = 15 + 3 * (m // GROUP - 1) + m % GROUP
-            prep = m % GROUP < PASSES and m < 3 * GROUP
-            for n in range(1 if m < 2 * GROUP else 0, COL_TILES):
+        for g in range(PASSES + 1):
+            if g < PASSES:
+                interleave(("phi", 2, g), 0)
+            if g >= 1:
+                quantize(("phi", 2, g - 1))
+
+        issued = 2 * GROUP
+        explained_rows = 0
+        for j in range(GROUP, len(order)):
+            while issued < min(j + PE_LEAD, len(order)):
                 for g in range(PASSES):
-                    mx_pass(m, n, g)
-            if prep:
-                interleave(c, S_LATE)
-            explain(m - 3)
-            if prep:
-                quantize(c)
-            for n in range(1 if m < 2 * GROUP else 0, COL_TILES):
-                drain(m, n)
-            store(m - 3)
-            if m % 2 == 0 and m // 2 + 1 < ROW_TILES // 2:
-                load_atoms(m // 2 + 1)
-        for m in range(ROW_TILES - 3, ROW_TILES):
-            store(m)
+                    mx_pass(*order[issued], g)
+                issued = issued + 1
+            drain(*order[j])
+            m, n = order[j]
+            step, phase = divmod(j - PREP_FIRST, PREP_STEP)
+            if phase == 0 and 0 <= step < PASSES:
+                interleave(("phi", 3, step), S_LATE)
+            if phase == 2 and 0 <= step < PASSES:
+                quantize(("phi", 3, step))
+            done_rows = m + 1 if n == COL_TILES - 1 else (m if m >= GROUP else 0)
+            if explained_rows < done_rows and j % 2 == 0:
+                explain(explained_rows)
+                explained_rows = explained_rows + 1
+            if n == COL_TILES - 1:
+                if m >= ROW_TILES - 2:
+                    store_tile(m)
+                elif m % 2 == 1:
+                    store_pair(m // 2)
+                if m in (3, 7):
+                    load_atoms(2 if m == 3 else 3)
+        for m in range(explained_rows, ROW_TILES):
             explain(m)
 
         shrink = keep.tile([P, ROW_TILES], F32)

@@ -1,7 +1,6 @@
 from contextlib import ExitStack
 
 import concourse.mybir as mybir
-from concourse.masks import make_identity
 
 N_ATOMS, N_SENSORS = 2048, 1536
 FLOPS = 2 * N_ATOMS * N_SENSORS * N_SENSORS
@@ -24,10 +23,11 @@ ROW_TILES = N_ATOMS // P
 COL_TILES = N_SENSORS // W
 GROUP = W // P
 HALF = N_ATOMS // 2
+SLOTS = HALF // P
 
 S_HEAD = 256
-S_MID = 160
-S_LATE = 384
+S_MID = 128
+S_LATE = 448
 PE_LEAD = 4
 PREP_FIRST = 16
 PREP_STEP = 4
@@ -40,6 +40,11 @@ def tile_sparse_bayes_posterior_variance_s2_kernel(
 
     def k_rows(first, second, g):
         return first[g * K_PASS : (g + 1) * K_PASS, :] if g < 2 else second
+
+    def tile_rows(tensor, m, count):
+        half, slot = divmod(m, SLOTS)
+        rows = tensor[half * HALF : (half + 1) * HALF, :].rearrange("(p e) s -> p e s", e=SLOTS)
+        return rows[:, slot : slot + count, :]
 
     def fmt(kind, g):
         return E5M2 if (kind == "prec" and g == 2) else E4M3
@@ -57,26 +62,27 @@ def tile_sparse_bayes_posterior_variance_s2_kernel(
             t = stream.tile([P, PACK, HALF], BF16, name="phi_raw", tag="phi_raw", bufs=6)
             rows = k_rows(phi_a, phi_b, g)[:, h * HALF : (h + 1) * HALF]
             nc.sync.dma_start(out=t[:], in_=rows.rearrange("(p j) w -> p j w", j=PACK))
+            by_slot = t[:].rearrange("p j (c e) -> p c j e", e=SLOTS)
             for b in range(2):
-                raw[("phi", 2 * h + b, g)] = t[:, :, b * W : (b + 1) * W]
+                raw[("phi", 2 * h + b, g)] = by_slot[:, :, :, b * GROUP : (b + 1) * GROUP]
 
         def load_prec(g):
             t = stream.tile([P, PACK, N_SENSORS], BF16, name="prec_raw", tag="wide_rows", bufs=4)
             nc.sync.dma_start(out=t[:], in_=k_rows(prec_a, prec_b, g).rearrange("(p j) w -> p j w", j=PACK))
             for n in range(COL_TILES):
-                raw[("prec", n, g)] = t[:, :, n * W : (n + 1) * W]
+                raw[("prec", n, g)] = t[:, :, n * W : (n + 1) * W].rearrange("p j (c i) -> p c j i", i=GROUP)
 
         def load_atoms(b):
             t = stream.tile([P, GROUP, N_SENSORS], BF16, name="atom_rows", tag="wide_rows", bufs=4)
-            rows = atoms[b * W : (b + 1) * W, :]
-            nc.sync.dma_start(out=t[:], in_=rows.rearrange("(h p) s -> p h s", p=P))
+            nc.sync.dma_start(out=t[:], in_=tile_rows(atoms, b * GROUP, GROUP))
             atom_rows[b] = t
 
         def interleave(chunk, s_cols):
             t = stream.tile([P, W, PACK], BF16, name="grouped", tag="grouped", bufs=4, align_bytes=64)
             v_cols = W - s_cols
-            src = raw[chunk].rearrange("p j (c i) -> p c j i", i=4)
-            dst = t[:].rearrange("p (c i) j -> p c j i", i=4)
+            src = raw[chunk]
+            layout = "p (i c) j -> p c j i" if chunk[0] == "phi" else "p (c i) j -> p c j i"
+            dst = t[:].rearrange(layout, i=GROUP)
             if s_cols > 0:
                 nc.scalar.copy(out=dst[:, v_cols // 4 :], in_=src[:, v_cols // 4 :])
             if v_cols > 0:
@@ -120,11 +126,10 @@ def tile_sparse_bayes_posterior_variance_s2_kernel(
             )
 
         def store_pair(q):
-            rows = out_0[2 * q * P : 2 * (q + 1) * P, :]
-            nc.sync.dma_start(out=rows.rearrange("(h p) s -> p h s", p=P), in_=gain[q][:])
+            nc.sync.dma_start(out=tile_rows(out_0, 2 * q, 2), in_=gain[q][:])
 
         def store_tile(m):
-            nc.sync.dma_start(out=out_0[m * P : (m + 1) * P, :], in_=gain[m // 2][:, m % 2, :])
+            nc.sync.dma_start(out=tile_rows(out_0, m, 1), in_=gain[m // 2][:, m % 2 : m % 2 + 1, :])
 
         def explain(m):
             products = stream.tile([P, N_SENSORS], F32, name="products", tag="products", bufs=2)
@@ -138,24 +143,16 @@ def tile_sparse_bayes_posterior_variance_s2_kernel(
                 accum_out=explained[:, m : m + 1],
             )
 
-        gamma_rows = keep.tile([ROW_TILES, P], BF16)
-        nc.scalar.dma_start(out=gamma_rows[:], in_=gamma.rearrange("(m p) -> m p", p=P))
+        gamma_rows = keep.tile([P, 2, SLOTS], BF16)
+        nc.scalar.dma_start(out=gamma_rows[:], in_=gamma.rearrange("(h p e) -> p h e", p=P, e=SLOTS))
         for g in range(PASSES):
             load_phi(0, g)
             load_prec(g)
         for g in range(PASSES):
             load_phi(1, g)
         load_atoms(0)
-        gamma_square = keep.tile([P, P], F32)
-        var_square = keep.tile([P, P], F32)
-        identity = keep.tile([P, P], F32)
-        nc.gpsimd.memset(gamma_square[:], 0.0)
-        make_identity(nc, identity[:])
-        nc.gpsimd.memset(var_square[:], 0.0)
-        nc.scalar.activation(out=gamma_square[:ROW_TILES, :], in_=gamma_rows[:], func=COPY)
-        gamma_turned = psum.tile([P, P], F32, name="bank", tag="bank")
-        nc.tensor.transpose(gamma_turned[:], gamma_square[:], identity[:])
         prior = keep.tile([P, ROW_TILES], F32)
+        nc.scalar.activation(out=prior[:], in_=gamma_rows[:].rearrange("p h e -> p (h e)"), func=COPY)
         explained = keep.tile([P, ROW_TILES], F32)
 
         head = []
@@ -169,8 +166,6 @@ def tile_sparse_bayes_posterior_variance_s2_kernel(
         for r in range(len(head) + 1):
             if r < len(head):
                 interleave(head[r], S_HEAD if r < len(head) - 2 else S_MID)
-            if r == 1:
-                nc.scalar.copy(out=prior[:], in_=gamma_turned[:, :ROW_TILES])
             if r >= 1:
                 quantize(head[r - 1])
                 kind, n, g = head[r - 1]
@@ -218,9 +213,6 @@ def tile_sparse_bayes_posterior_variance_s2_kernel(
 
         shrink = keep.tile([P, ROW_TILES], F32)
         nc.vector.tensor_tensor(out=shrink[:], in0=explained[:], in1=prior[:], op=ALU.mult)
-        nc.vector.tensor_tensor(out=var_square[:, :ROW_TILES], in0=prior[:], in1=shrink[:], op=ALU.subtract)
-        var_turned = psum.tile([P, P], F32, name="bank", tag="bank")
-        nc.tensor.transpose(var_turned[:], var_square[:], identity[:])
-        var_rows = keep.tile([ROW_TILES, P], F32)
-        nc.scalar.copy(out=var_rows[:], in_=var_turned[:ROW_TILES, :])
-        nc.scalar.dma_start(out=out_1.rearrange("(m p) -> m p", p=P), in_=var_rows[:])
+        var = keep.tile([P, 2, SLOTS], F32)
+        nc.vector.tensor_tensor(out=var[:].rearrange("p h e -> p (h e)"), in0=prior[:], in1=shrink[:], op=ALU.subtract)
+        nc.scalar.dma_start(out=out_1.rearrange("(h p e) -> p h e", p=P, e=SLOTS), in_=var[:])

from contextlib import ExitStack

import concourse.mybir as mybir

N_ATOMS, N_SENSORS = 2048, 1536
FLOPS = 2 * N_ATOMS * N_SENSORS * N_SENSORS

F32 = mybir.dt.float32
BF16 = mybir.dt.bfloat16
U32 = mybir.dt.uint32
U8 = mybir.dt.uint8
E4M3 = mybir.dt.float8_e4m3fn_x4
E5M2 = mybir.dt.float8_e5m2_x4
ALU = mybir.AluOpType
COPY = mybir.ActivationFunctionType.Copy

P = 128
PACK = 4
K_PASS = P * PACK
PASSES = 3
W = 512
ROW_TILES = N_ATOMS // P
COL_TILES = N_SENSORS // W
GROUP = W // P
HALF = N_ATOMS // 2
SLOTS = HALF // P

S_HEAD = 256
S_MID = 128
S_LATE = 448
PE_LEAD = 4
PREP_FIRST = 16
PREP_STEP = 4


def tile_sparse_bayes_posterior_variance_s2_kernel(
    tc, phi_a, phi_b, prec_a, prec_b, atoms, gamma, out_0, out_1
):
    nc = tc.nc

    def k_rows(first, second, g):
        return first[g * K_PASS : (g + 1) * K_PASS, :] if g < 2 else second

    def tile_rows(tensor, m, count):
        half, slot = divmod(m, SLOTS)
        rows = tensor[half * HALF : (half + 1) * HALF, :].rearrange("(p e) s -> p e s", e=SLOTS)
        return rows[:, slot : slot + count, :]

    def fmt(kind, g):
        return E5M2 if (kind == "prec" and g == 2) else E4M3

    with ExitStack() as ctx:
        keep = ctx.enter_context(tc.tile_pool(name="keep", bufs=1))
        stream = ctx.enter_context(tc.tile_pool(name="stream", bufs=1))
        psum = ctx.enter_context(tc.psum_pool(name="psum", bufs=8))
        ctx.enter_context(tc.manual_schedule())

        raw, grouped, codes, scales = {}, {}, {}, {}
        atom_rows, gain, acc = {}, {}, {}

        def load_phi(h, g):
            t = stream.tile([P, PACK, HALF], BF16, name="phi_raw", tag="phi_raw", bufs=6)
            rows = k_rows(phi_a, phi_b, g)[:, h * HALF : (h + 1) * HALF]
            nc.sync.dma_start(out=t[:], in_=rows.rearrange("(p j) w -> p j w", j=PACK))
            by_slot = t[:].rearrange("p j (c e) -> p c j e", e=SLOTS)
            for b in range(2):
                raw[("phi", 2 * h + b, g)] = by_slot[:, :, :, b * GROUP : (b + 1) * GROUP]

        def load_prec(g):
            t = stream.tile([P, PACK, N_SENSORS], BF16, name="prec_raw", tag="wide_rows", bufs=4)
            nc.sync.dma_start(out=t[:], in_=k_rows(prec_a, prec_b, g).rearrange("(p j) w -> p j w", j=PACK))
            for n in range(COL_TILES):
                raw[("prec", n, g)] = t[:, :, n * W : (n + 1) * W].rearrange("p j (c i) -> p c j i", i=GROUP)

        def load_atoms(b):
            t = stream.tile([P, GROUP, N_SENSORS], BF16, name="atom_rows", tag="wide_rows", bufs=4)
            nc.sync.dma_start(out=t[:], in_=tile_rows(atoms, b * GROUP, GROUP))
            atom_rows[b] = t

        def interleave(chunk, s_cols):
            t = stream.tile([P, W, PACK], BF16, name="grouped", tag="grouped", bufs=4, align_bytes=64)
            v_cols = W - s_cols
            src = raw[chunk]
            layout = "p (i c) j -> p c j i" if chunk[0] == "phi" else "p (c i) j -> p c j i"
            dst = t[:].rearrange(layout, i=GROUP)
            if s_cols > 0:
                nc.scalar.copy(out=dst[:, v_cols // 4 :], in_=src[:, v_cols // 4 :])
            if v_cols > 0:
                nc.vector.tensor_copy(out=dst[:, : v_cols // 4], in_=src[:, : v_cols // 4])
            grouped[chunk] = t

        def quantize(chunk):
            kind, b, g = chunk
            cw = keep.tile([P, W], U32, name="codes_%s_%d_%d" % chunk, align_bytes=64)
            sc = keep.tile([P, W], U8, name="scales_%s_%d_%d" % chunk, align_bytes=64)
            nc.vector.quantize_mx(
                out=cw[:].bitcast(fmt(kind, g)),
                scales=sc[:],
                in_=grouped[chunk][:].rearrange("p w j -> p (w j)"),
            )
            codes[chunk], scales[chunk] = cw, sc

        def mx_pass(m, n, g):
            if g == 0:
                acc[(m, n)] = psum.tile([P, W], F32, name="bank", tag="bank")
            left, right = ("phi", m // GROUP, g), ("prec", n, g)
            cols = slice((m % GROUP) * P, (m % GROUP + 1) * P)
            nc.tensor.matmul_mx(
                out=acc[(m, n)][:],
                lhsT=codes[left][:, cols].bitcast(E4M3),
                lhsT_scale=scales[left][:, cols],
                rhs=codes[right][:].bitcast(fmt("prec", g)),
                rhs_scale=scales[right][:],
                start=(g == 0),
                stop=(g == PASSES - 1),
            )

        def drain(m, n):
            if n == 0 and m % 2 == 0:
                gain[m // 2] = stream.tile([P, 2, N_SENSORS], F32, name="gain", tag="gain", bufs=4)
            nc.scalar.activation(
                out=gain[m // 2][:, m % 2, n * W : (n + 1) * W],
                in_=acc[(m, n)][:],
                func=COPY,
                scale=prior[:, m : m + 1],
            )

        def store_pair(q):
            nc.sync.dma_start(out=tile_rows(out_0, 2 * q, 2), in_=gain[q][:])

        def store_tile(m):
            nc.sync.dma_start(out=tile_rows(out_0, m, 1), in_=gain[m // 2][:, m % 2 : m % 2 + 1, :])

        def explain(m):
            products = stream.tile([P, N_SENSORS], F32, name="products", tag="products", bufs=2)
            nc.vector.scalar_tensor_tensor(
                out=products[:],
                in0=gain[m // 2][:, m % 2, :],
                scalar=1.0,
                in1=atom_rows[m // GROUP][:, m % GROUP, :],
                op0=ALU.mult,
                op1=ALU.mult,
                accum_out=explained[:, m : m + 1],
            )

        gamma_rows = keep.tile([P, 2, SLOTS], BF16)
        nc.scalar.dma_start(out=gamma_rows[:], in_=gamma.rearrange("(h p e) -> p h e", p=P, e=SLOTS))
        for g in range(PASSES):
            load_phi(0, g)
            load_prec(g)
        for g in range(PASSES):
            load_phi(1, g)
        load_atoms(0)
        prior = keep.tile([P, ROW_TILES], F32)
        nc.scalar.activation(out=prior[:], in_=gamma_rows[:].rearrange("p h e -> p (h e)"), func=COPY)
        explained = keep.tile([P, ROW_TILES], F32)

        head = []
        for g in range(PASSES - 1):
            head.extend([("phi", 0, g), ("phi", 1, g)] + [("prec", n, g) for n in range(COL_TILES)])
        head.extend([("phi", 0, 2)] + [("prec", n, 2) for n in range(COL_TILES)] + [("phi", 1, 2)])

        order = [(m, n) for n in range(COL_TILES) for m in range(GROUP)]
        order.extend([(m, n) for m in range(GROUP, ROW_TILES) for n in range(COL_TILES)])

        for r in range(len(head) + 1):
            if r < len(head):
                interleave(head[r], S_HEAD if r < len(head) - 2 else S_MID)
            if r >= 1:
                quantize(head[r - 1])
                kind, n, g = head[r - 1]
                if kind == "prec" and n < 2:
                    for m in range(GROUP):
                        mx_pass(m, n, g)
            if r in (len(head) - 2, len(head) - 1):
                drain(*order[2 * (r - len(head) + 2)])
                drain(*order[2 * (r - len(head) + 2) + 1])
        load_atoms(1)

        for g in range(PASSES + 1):
            if g < PASSES:
                interleave(("phi", 2, g), 0)
            if g >= 1:
                quantize(("phi", 2, g - 1))

        issued = 2 * GROUP
        explained_rows = 0
        for j in range(GROUP, len(order)):
            while issued < min(j + PE_LEAD, len(order)):
                for g in range(PASSES):
                    mx_pass(*order[issued], g)
                issued = issued + 1
            drain(*order[j])
            m, n = order[j]
            step, phase = divmod(j - PREP_FIRST, PREP_STEP)
            if phase == 0 and 0 <= step < PASSES:
                interleave(("phi", 3, step), S_LATE)
            if phase == 2 and 0 <= step < PASSES:
                quantize(("phi", 3, step))
            done_rows = m + 1 if n == COL_TILES - 1 else (m if m >= GROUP else 0)
            if explained_rows < done_rows and j % 2 == 0:
                explain(explained_rows)
                explained_rows = explained_rows + 1
            if n == COL_TILES - 1:
                if m >= ROW_TILES - 2:
                    store_tile(m)
                elif m % 2 == 1:
                    store_pair(m // 2)
                if m in (3, 7):
                    load_atoms(2 if m == 3 else 3)
        for m in range(explained_rows, ROW_TILES):
            explain(m)

        shrink = keep.tile([P, ROW_TILES], F32)
        nc.vector.tensor_tensor(out=shrink[:], in0=explained[:], in1=prior[:], op=ALU.mult)
        var = keep.tile([P, 2, SLOTS], F32)
        nc.vector.tensor_tensor(out=var[:].rearrange("p h e -> p (h e)"), in0=prior[:], in1=shrink[:], op=ALU.subtract)
        nc.scalar.dma_start(out=out_1.rearrange("(h p e) -> p h e", p=P, e=SLOTS), in_=var[:])
